import numpy as np, ml_dtypes
CORES = [3,11,19,27,35,43,51,59]
N = 8
import mx_ref
BF = ml_dtypes.bfloat16
def tile(rs):
    return np.stack(rs, axis=2).reshape(128, -1).astype(BF)
def pick(q, e):
    c = np.concatenate([q[0].reshape(128, -1, 4), np.zeros((128, 1, 4), np.uint8)], axis=1); s = np.concatenate([q[1], np.ones((16, 1), np.uint8)], axis=1)
    return (np.ascontiguousarray(c[:, e].reshape(128, -1)), np.ascontiguousarray(s[:, e]))
def join(*qs):
    return (np.concatenate([q[0] for q in qs], axis=1), np.concatenate([q[1] for q in qs], axis=1))
def put(q, e, v):
    c, s = q[0].reshape(128, -1, 4).copy(), q[1].copy(); c[:, e] = v[0].reshape(128, -1, 4); s[:, e] = v[1]
    return (c.reshape(128, -1), s)
def pk(c, s):
    return (np.ascontiguousarray(c), mx_ref.live(s))
def emit(q):
    return q[0], q[1]
def packed(v, rng):
    q = [mx_ref.quantize(np.ascontiguousarray(v[r])) for r in range(N)]
    return np.stack([a for a, b in q]), np.stack([mx_ref.plane(b, rng) for a, b in q])
def values_of_codes():
    e, c = np.zeros((128, 128, 4), np.float32), np.zeros((128, 2, 4), np.uint8)
    e[np.arange(128), np.arange(128), 0] = 1
    c[:127, :, 0] = np.arange(256).reshape(2, 128).T[:127]
    return mx_ref.matmul(mx_ref.quantize(e.reshape(128, 512).astype(BF)), (c.reshape(128, 8), np.full((16, 2), 127, np.uint8))).T.reshape(-1).astype(np.float64)
CODE_VALUE, SCALE_VALUE = values_of_codes(), 2.0 ** (np.arange(256) - 127.0)
def decode(q):
    return (CODE_VALUE[q[0]].reshape(16, 8, -1, 4) * SCALE_VALUE[q[1]][:, None, :, None] + 0.0).reshape(128, -1).astype(np.float32)
def f(rng, *shape):
    return mx_ref.flush((rng.standard_normal(shape, dtype=np.float32) * np.exp2(rng.integers(-2, 3, shape[:-1] + (1,)))).astype(BF))
def wide(rng, *shape, cols=0):
    v = rng.standard_normal(shape, dtype=np.float32) * np.exp2(rng.integers(-12, 13, shape)).astype(np.float32)
    if cols: v *= np.repeat(np.exp2(rng.integers(-cols, cols + 1, shape[:-2] + (1, shape[-1] // 4))) * (rng.random(shape[:-2] + (1, shape[-1] // 4)) > 0.0625), 4, axis=-1).astype(np.float32)
    return mx_ref.flush(v.astype(BF))
C, A, R = 256, 128, 3
def numbers_of(rng):
    return {"x": np.array(f(rng, N, 128, 4 * C)), "u": np.array(f(rng, N, 128, 512)), "v": np.array(f(rng, N, 128, 512))}
def layers(rng):
    return np.array(f(rng, N, 128, 2048)).reshape(N, 8, 16, 4, 8, 16, 4)
def weights(rng, w):
    c, s = packed(np.ascontiguousarray(w).reshape(N, 128, 2048), rng)
    return {"wc": c, "ws": s}
def setup_inputs(rng):
    return {**numbers_of(rng), **weights(rng, layers(rng))}
def setup_inputs_ties(rng):
    d = numbers_of(rng)
    x = d["x"].reshape(N, 8, 16, C, 4)
    u = d["u"].reshape(N, 128, 128, 4)
    e = rng.permutation(N)
    for i, r in enumerate(e):
        k = np.arange(C) % 3
        if i % 2 == 0: k = k[rng.permutation(C)]
        if i == 0: k = np.zeros(C, int)
        a = x[r][:, :8, :3].copy()
        a[:, :, 2] = 0
        x[r][:, :8] = a[:, :, k]
        if i % 4 in (0, 3):
            u[r][:, ::16] = u[r][:, :1].copy()
            u[r][:, 1::16] = u[r][:, 1:2].copy()
    x[e[1]] = 0
    h = u.reshape(N, 8, 16, 128, 4)
    h[:, :, 8:, ::16] = 0
    h[:, :, 8:, 1::16] = 0
    w = layers(rng)
    w[:, :, :, :, :, :8] = 0
    return {"x": x.reshape(N, 128, 4 * C), "u": u.reshape(N, 128, 512), "v": d["v"], **weights(rng, w)}
def setup_inputs_near(rng):
    d = numbers_of(rng)
    x = d["x"].astype(np.float32).reshape(N, 8, 16, C, 4)
    u = d["u"].reshape(N, 128, 128, 4)
    u[:, :, ::16] = 0
    u[:, :, 1::16] = 0
    x[:, :, 0] = 0
    x[:, :, 8:] = 0
    o = rng.permutation(N) % 4
    for r in range(N):
        k = 1.0 if o[r] == 0 else 2.0 ** -30
        if o[r] < 3: x[r, :, 8] = ((rng.integers(0, 16, (8, C))[:, :, None] >> np.arange(4)) & 1) * np.exp2(np.arange(4) - 23.0)
        if o[r] < 2:
            x[r, :, 0, :, 0] = rng.integers(0, 2, (8, C)) * 2.0 - 1.0
            x[r, :, 11, :, 0] = 2.0 ** -10
        if o[r] == 2:
            for g in rng.permutation(8)[:4]: x[r, g, 0, rng.integers(C), 0] = 2.0 ** 16 * rng.choice([-1.0, 1.0])
        if o[r] == 3:
            s = rng.integers(0, 2, (8, C)) * 0.125
            x[r, :, 10, :, 0] = (1.0 + s) * 2.0 ** -30
            x[r, :, 12, :, 0] = (1.125 - s) * 2.0 ** -30
        for h in range(0, 128, 16):
            for c, a in ((h, h), (h + 1, (h + 16) % 128)):
                if o[r] < 3:
                    u[r, a, c, 0] = 2.0 ** 30 if o[r] == 2 else k
                    u[r, a + 8, c] = k
                if o[r] < 2: u[r, a + 11, c, 0] = k
                if o[r] == 3:
                    u[r, a + 10, c, 0] = 1.25 * k
                    u[r, a + 12, c, 0] = 1.125 * k
    w = layers(rng)
    for i in [0] + [8 + j for j in range(8)]:
        w[:, :, i] = 0
        w[:, :, :, :, :, i] = 0
    return {"x": x.reshape(N, 128, 4 * C).astype(BF), "u": u.reshape(N, 128, 512), "v": d["v"], **weights(rng, w)}
def setup_inputs_ends(rng):
    d = numbers_of(rng)
    o = (np.arange(N) + rng.integers(N)) % 4
    x = np.zeros((N, 8, 16, C, 4), np.float32)
    u = d["u"].reshape(N, 128, 128, 4)
    for r in range(N):
        a = 2.0 ** 30 * (1.0 - 0.1 * rng.random((128, 8, 2, 4)))
        if o[r] == 0:
            x[r] = -2.0 ** 29 * (0.8 + 0.075 * rng.random((8, 16, C, 4)))
            a[:, :, 0] *= np.exp2(-1.0 * np.concatenate([rng.permutation(4), rng.permutation(4)]))[:, None]
            d["v"][r] = (2.0 ** 30 * rng.choice([-1.0, 1.0], (128, 512))).astype(np.float32).astype(BF)
        if o[r] == 1:
            x[r] = 2.0 ** 29 * np.where((rng.permutation(C) % 2 == 0)[:, None], 0.875, -0.7 - 0.07 * rng.random((8, 16, C, 4)))
            a *= rng.choice([-1.0, 1.0], (8, 2))[None, :, :, None]
        if o[r] == 2:
            x[r] = 2.0 ** -30 * rng.choice([-1.0, 1.0], (8, 16, C, 4))
            a = 2.0 ** -30 * rng.choice([-1.0, 1.0], (128, 8, 2, 4))
            a[0, :, :, 0] = 0
            d["v"][r] = (2.0 ** -30 * rng.choice([-1.0, 1.0], (128, 512))).astype(np.float32).astype(BF)
        if o[r] == 3:
            x[r] = (1.0 + rng.random((8, 16, 1, 4))) * rng.choice([-1.0, 1.0], (8, 16, 1, 4))
            a = (1.0 + rng.random((128, 1, 2, 4))) * rng.choice([-1.0, 1.0], (128, 1, 2, 4)) * np.ones((1, 8, 1, 1))
        a = a.astype(np.float32).astype(BF)
        u[r][:, ::16] = a[:, :, 0]
        u[r][:, 1::16] = a[:, :, 1]
    w = np.zeros((N, 128, 4, 128, 4), np.float32)
    i = np.arange(128)
    for b in range(4): w[:, i, b, i, b] = 2
    return {"x": x.reshape(N, 128, 4 * C).astype(BF), "u": u.reshape(N, 128, 512), "v": d["v"], **weights(rng, w.astype(BF))}
def setup_inputs_odd(rng):
    d = numbers_of(rng)
    k = (N, 8, 16, C, 4)
    x = (129.0 + 2.0 * rng.integers(0, 64, k)) * np.exp2(rng.integers(-21, -14, k)) * rng.choice([-1.0, 1.0], k)
    x[:, :, ::8] = 0
    x[:, :, ::8, :, 0] = np.where(rng.random((N, 8, 2, C)) < 0.5, 1.96875, 1.875)
    w = layers(rng)
    w[:, :, ::8] = 0
    w[:, :, :, :, :, ::8] = 0
    return {"x": x.astype(np.float32).reshape(N, 128, 4 * C).astype(BF), "u": d["u"], "v": d["v"], **weights(rng, w)}
def setup_inputs_spread(rng):
    d = setup_inputs(rng)
    d["x"] = np.clip(wide(rng, N, 128, 4 * C, cols=2).astype(np.float32), -65536.0, 65536.0).astype(BF)
    return d
def check_inputs(d):
    b = []
    for k in ("x", "u", "v"):
        a = np.abs(d[k].astype(np.float32))
        if not (np.isfinite(a).all() and ((a == 0) | (a >= 2.0 ** -30) & (a <= 2.0 ** 30)).all()): b.append("a value of " + k)
    none, least, most = [emit(mx_ref.quantize(np.full((128, 16), k, np.float32).astype(BF)))[1][0, 0] for k in (0.0, 2.0 ** -30, 2.0 ** 30)]
    total = 0.0
    for r in range(N):
        if ((d["wc"][r] == 0x7F) | (d["wc"][r] == 0xFF)).any(): b.append("wc: a code that is no number")
        s = mx_ref.live(d["ws"][r])
        if ((s != none) & ((s < least) | (s > most))).any(): b.append("ws: a scale out of range")
        w = np.abs(decode(pk(d["wc"][r], d["ws"][r])).astype(np.float64)).reshape(128, 512, 4)
        total = max(total, float(np.max(np.sum(w, axis=(0, 2)))))
    a = float(np.max(np.abs(d["x"].astype(np.float32))))
    if not a * (1.0 + total * 0.015625) ** 3 <= 2.0 ** 29: b.append("x and W: a * (1 + s)**3")
    return b
def departures(s):
    half = np.argsort(-s[::16].reshape(2, 4 * C), axis=1, kind="stable") // C
    leaf = np.argsort(-s[1::16], axis=1, kind="stable")
    e = np.zeros((8, C), np.int64)
    for g in range(8): e[g, leaf[g]] = 2 * np.flatnonzero(half[g // 4] == g % 4) + g // 4
    return e.reshape(-1)
def reference(x, u, v, wc, ws):
    qu = [mx_ref.quantize(u[r]) for r in range(N)]
    lay = [pk(wc[r], ws[r]) for r in range(N)]
    now = [x[r] for r in range(N)]
    for t in range(R):
        own, dep, sent = [], [], []
        for r in range(N):
            q = mx_ref.quantize(now[r])
            dep.append(departures(mx_ref.matmul(qu[r], q) + np.float32(0.0)))
            own.append(decode(q).reshape(8, 16, C, 4).transpose(0, 2, 1, 3).reshape(8 * C, 16, 4))
            p = own[r][np.argsort(dep[r])]
            e = ((p[:4 * C] + p[4 * C:]) * np.float32(0.5)).astype(BF)
            sent.append(mx_ref.quantize(np.ascontiguousarray(e.reshape(A, 8, 16, 4).transpose(1, 2, 0, 3)).reshape(128, 4 * A)))
        for r in range(N):
            q = sent[r - 1]
            h = tile([mx_ref.matmul(pick(lay[r], np.arange(128 * b, 128 * b + 128)), q) * np.float32(0.015625) for b in range(4)])
            h = h.reshape(8, 16, A, 4).transpose(2, 0, 1, 3).reshape(8 * A, 16, 4).astype(np.float32)
            z = (own[r] + h[dep[r] % (4 * C)]).astype(BF)
            now[r] = np.ascontiguousarray(z.reshape(8, C, 16, 4).transpose(0, 2, 1, 3)).reshape(128, 4 * C)
    y, op = np.zeros((N, 128, C), np.float32), np.zeros((N, 8, C), np.float32)
    oc, osc = np.zeros((N, 128, 4 * C), np.uint8), np.zeros((N, 16, C), np.uint8)
    for r in range(N):
        q = mx_ref.quantize(now[r])
        y[r] = mx_ref.matmul(mx_ref.quantize(v[r]), q)
        op[r] = dep[r].reshape(8, C)
        oc[r], osc[r] = emit(q)
    return {"y": y, "op": op, "oc": oc, "osc": osc}

@@ -1,0 +1,493 @@
+from concourse.mybir import dt, AluOpType as A, ActivationFunctionType as F
+import comms_topo
+
+R = 3
+SCRATCH = {}
+SEMAPHORES = ["sV", "sS", "sP", "sG", "ls"] + ["arr%d" % t for t in range(R)] + ["lst%d" % t for t in range(R)] + ["d%d" % i for i in range(40)]
+
+
+def _b(name, n, d, where="sbuf"):
+    SCRATCH[name] = (where, [128, n], d)
+
+
+def _q(name, n):
+    _b(name, n, "float8_e4m3fn_x4")
+    _b(name + "_s", n, "uint8")
+
+
+for _t in range(R):
+    _q("qx%d" % _t, 768)
+    _q("land%d" % _t, 256)
+    _b("lin%d" % _t, 64, "uint16")
+    _b("el%d" % _t, 64, "uint16")
+for _n, _w in (("qx3", 256), ("qn", 256), ("qu", 128), ("qr", 2048), ("qv", 128), ("wq", 512), ("qwr", 2048), ("cc", 1024),
+               ("cid", 512), ("cwn", 2048), ("ke", 128), ("m2q", 1024), ("mq", 4096), ("qw", 256), ("qe", 128)):
+    _q(_n, _w)
+for _n, _w in (("xb", 1024), ("xs", 1024), ("xn", 1024), ("ub", 512), ("vb", 512), ("zero", 1024), ("cst", 4096), ("zc", 2600),
+               ("kb", 512), ("onesb", 128), ("halfb", 128), ("negb", 256), ("thr0", 256), ("thr1", 256), ("mt", 8192), ("m2", 4096),
+               ("dd", 8192), ("win", 4096), ("winh", 2048), ("fx", 1024), ("etmp", 512), ("eb", 512), ("ww", 1024),
+               ("ab", 256), ("da", 256), ("dn", 256), ("dat", 256)):
+    _b(_n, _w, "bfloat16")
+for _n in ("mk16", "rs16", "mk4", "rs4", "msk", "scn", "psb", "awin", "it16", "it4", "dfull", "ysb", "cols", "itb", "leaf"):
+    _b(_n, 256, "float32")
+_b("lw", 1024, "float32")
+_b("cf", 8, "float32")
+_b("kc", 16, "float32")
+for _n, _w in (("ci", 8), ("il", 128), ("il2", 128), ("il3", 128), ("xi", 64), ("xi2", 64), ("xi3", 64)):
+    _b(_n, _w, "int32")
+for _n, _w in (("ulist", 128), ("wlist", 128), ("n1l", 16), ("n2l", 16), ("pl", 16), ("ql", 16), ("xl", 64)):
+    _b(_n, _w, "uint16")
+SCRATCH["ld"] = ("dram", [32, 1024], "float32")
+_b("pr0", 1024, "float32", "psum")
+_b("pr1", 1024, "float32", "psum")
+for _k in range(4, 8):
+    _b("pb%d" % _k, 512, "float32", "psum")
+
+
+def rank_program(g, core, T, topo):
+    rank = T.rank_of(core)
+    if rank is None:
+        return
+    nxt = T.cores[(rank + 1) % len(T.cores)]
+    prv = T.cores[(rank - 1) % len(T.cores)]
+    rid, pid, _se = topo.addr(nxt)
+    mask = topo.mask(core, nxt)
+    n_eng = len(topo.engines(core, nxt))
+    n_in = len(topo.engines(prv, core))
+
+    eng = {"V": g.vector, "S": g.scalar, "P": g.tensor, "G": g, "Y": g.sync}
+    cnt = {"V": 0, "S": 0, "P": 0, "G": 0}
+    waited = {e: {} for e in eng}
+    lastw, readers, total = {}, {}, {}
+    ndma, nrem = [0], [0]
+
+    def need(e, reads, writes, acc=False):
+        w = {}
+        own = "s" + e
+
+        def add(sv):
+            if w.get(sv[0], 0) < sv[1]:
+                w[sv[0]] = sv[1]
+        for k in reads:
+            if k in lastw:
+                add(lastw[k])
+            if k[0] == "K":
+                for sv in readers.get(k, ()):
+                    if sv[0] != own:
+                        add(sv)
+        for k in writes:
+            if k in lastw and not (acc and lastw[k][0] == own):
+                add(lastw[k])
+            for sv in readers.get(k, ()):
+                if sv[0] != own:
+                    add(sv)
+        for s, v in w.items():
+            if waited[e].get(s, 0) < v:
+                eng[e].wait_ge(T.sem[s], v)
+                waited[e][s] = v
+
+    def note(sv, reads, writes):
+        for k in reads:
+            readers.setdefault(k, []).append(sv)
+        for k in writes:
+            lastw[k] = sv
+            readers[k] = []
+        total[sv[0]] = max(total.get(sv[0], 0), sv[1])
+
+    def op(e, fn, args, reads, writes, acc=False, **kw):
+        need(e, reads, writes, acc)
+        cnt[e] += 1
+        fn(*args, **kw).then_inc(T.sem["s" + e], 1)
+        note(("s" + e, cnt[e]), reads, writes)
+
+    def dmas(e, pairs, reads, writes):
+        need(e, reads, writes)
+        s = "d%d" % ndma[0]
+        ndma[0] += 1
+        for out, in_ in pairs:
+            eng[e].dma_start(out, in_).then_inc(T.sem[s], 16)
+        note((s, 16 * len(pairs)), reads, writes)
+
+    def remote(out, in_, sem, reads):
+        need("G", reads, [])
+        g.remote_dma(out, in_, T.sem[sem], T.sem.ls, pid, rid, mask)
+        nrem[0] += 1
+
+    V, S, P = g.vector, g.scalar, g.tensor
+
+    def cv(name, a, b):
+        return T[name][:, a:b].bitcast(dt.uint8)
+
+    def quant(name, a, b, src, key, reads, s0=0):
+        op("V", V.quantize_mx, (T[name][:, a:b], T[name + "_s"][:, a:b], T[src][:, s0:s0 + 4 * (b - a)]), reads, [key])
+
+    def bank(k, n):
+        if k < 4:
+            return T["pr%d" % (k // 2)][:, 512 * (k % 2):512 * (k % 2) + n]
+        return T["pb%d" % k][:, 0:n]
+
+    def mm(k, n, l, la, r, ra, start, stop, reads):
+        op("P", P.matmul_mx, (bank(k, n), T[l][:, la:la + 128], T[l + "_s"][:, la:la + 128],
+                              T[r][:, ra:ra + n], T[r + "_s"][:, ra:ra + n], start, stop),
+           reads, [("K", k)], acc=not start)
+
+    def ts(out, in0, s1, o0, reads, writes, s2=None, o1=None):
+        op("V", V.tensor_scalar, (out, in0, s1, s2, o0) if o1 is None else (out, in0, s1, s2, o0, o1), reads, writes)
+
+    def tt(out, a, b, o, reads, writes):
+        op("V", V.tensor_tensor, (out, a, b, o), reads, writes)
+
+    def vcopy(out, in_, reads, writes):
+        op("V", V.tensor_copy, (out, in_), reads, writes)
+
+    def act(out, in_, f, reads, writes, **kw):
+        op("S", S.activation, (out, in_, f), reads, writes, **kw)
+
+    def memset(ap, c, writes, reads=()):
+        op("V", V.memset, (ap, c), list(reads), writes)
+
+    def iota(name, pat, base, cm):
+        op("G", g.iota, (T[name][:], pat, base, cm), [], [name], allow_small_or_imprecise_dtypes=True)
+
+    def select(out, in_, pat, cmp, base, cm, reads, writes):
+        op("G", g.affine_select, (out, in_, pat, cmp, 0.0, base, cm), reads, writes)
+
+    dmas("S", [(T.ub[:], T.u[:, :])], [], ["ub"])
+    dmas("Y", [(T.xb[:], T.x[:, :])], [], ["xb"])
+    dmas("Y", [(cv("wq", 0, 512), T.wc[:, :])], [], ["wq"])
+    dmas("Y", [(T.wq_s[:], T.ws[:, :])], [], ["wqs"])
+    dmas("Y", [(T.vb[:], T.v[:, :])], [], ["vb"])
+
+    iota("il", [[1, 2], [16, 8], [0, 8]], 0, 0)
+    iota("ci", [[0, 8]], 0, 1)
+    memset(T.zero[:], 0.0, ["zero"])
+    memset(T.negb[:], -2.0 ** -120, ["negb"])
+    memset(T.onesb[:], 1.0, ["onesb"])
+    memset(T.halfb[:], 0.5, ["halfb"])
+    vcopy(T.ulist[:], T.il[:], ["il"], ["ulist"])
+    for b in range(2):
+        select(T["thr%d" % b][:], T.negb[:], [[1, 256]], A.is_ge, -1 - 128 * b, -1, ["negb"], ["thr%d" % b])
+    for i in range(3):
+        act(T.zc[:, 1024 * i:min(2600, 1024 * i + 1024)], T.zero[:, 0:min(1024, 2600 - 1024 * i)], F.Copy, ["zero"], ["zz%d" % i])
+    zz = ["zz0", "zz1", "zz2"]
+    select(T.zc[:, 2084:2596:4], T.onesb[:], [[-1, 128]], A.is_equal, 0, 1, ["onesb"] + zz, ["zc4"])
+    for s in range(4):
+        select(T.zc[:, s * 520 + 4:s * 520 + 516:4], T.halfb[:], [[0, 4], [-64, 2], [-1, 16]], A.is_equal, -16 * s, 1, ["halfb"] + zz, ["zc%d" % s])
+    quant("qx0", 0, 256, "zero", "z0", ["zero"])
+    quant("qx0", 512, 768, "zero", "z0b", ["zero"])
+    quant("qu", 0, 128, "ub", "qu", ["ub"])
+
+    def pick_u(a):
+        lst = T.ulist[:, a // 16:a // 16 + 32]
+        vcopy(T.qr[:, a:a + 512].bitcast(dt.uint32), T.qu[:, 0:128].bitcast(dt.uint32).indirect(lst), ["qu", "ulist"], [("qr", a // 512)])
+        act(T.qr_s[:, a:a + 512], T.qu_s[:, 0:128].indirect(lst), F.Copy, ["qu", "ulist"], [("qrs", a // 512)])
+    pick_u(0)
+    quant("qx0", 256, 512, "xb", ("qx", 0), ["xb"])
+    act(T.xn[:], T.xb[:], F.Copy, ["xb"], ["xn"], scale=-1.0)
+    pick_u(1024)
+    pick_u(512)
+    pick_u(1536)
+    for i in range(4):
+        act(T.cst[:, 1024 * i:1024 * i + 1024], T.zero[:], F.Copy, ["zero"], ["cst%d" % (9 + i)])
+    for c, sh, an in ((1, 0, 15), (2, 2, 3), (3, 0, 3), (4, 4, 3), (5, 0, 1), (6, 6, 1)):
+        ts(T.ci[:, c:c + 1], T.ci[:, 0:1], sh, A.logical_shift_right, ["ci"], ["ci%d" % c], an, A.bitwise_and)
+    vcopy(T.cf[:, 0:7], T.ci[:, 0:7], ["ci"] + ["ci%d" % c for c in range(1, 7)], ["cf"])
+
+    def col(c):
+        return T.cf[:, c:c + 1]
+
+    def kc(c):
+        return T.kc[:, c:c + 1]
+
+    def qrk(s, gr):
+        i = (8 * s + gr) // 4
+        return [("qr", i), ("qrs", i)]
+
+    def setup_late():
+        iota("it16", [[0, 16], [1, 16]], 0, 0)
+        iota("it4", [[0, 64], [1, 4]], 0, 0)
+        for nm, q in (("rs16", 16), ("rs4", 4)):
+            iota(nm, [[0, 256]], 1, 0)
+            select(T[nm][:], T[nm][:], [[0, 256 // q], [1, q]], A.not_equal, 0, 0, [nm], [nm])
+        iota("itb", [[1, 256]], 0, 0)
+        iota("il2", [[32, 16], [16, 2], [0, 4]], 0, 0)
+        memset(T.cst[:, 448:512], 1.0, ["cst8"], ["cst9"])
+        for t in range(4):
+            o = 1024 * (1 + t // 2) + 448
+            memset(T.cst[:, o + t:o + 64:4], 1.0, ["cst%d" % t], ["cst10", "cst11"])
+            o = 3072 + 448 + 64 * (t // 2)
+            memset(T.cst[:, o + t:o + 64:4], 1.0 - 0.5 * (t % 2), ["cst%d" % (4 + t)], ["cst12"])
+        for i in range(2):
+            quant("cc", 512 * i, 512 * i + 512, "cst", "cc%d" % i, ["cst%d" % t for t in range(13)], s0=2048 * i)
+        for s in range(4):
+            for b in range(4):
+                a = 128 * (4 * s + b)
+                quant("cwn", a, a + 128, "zc", ("cwn", s, b), zz + ["zc%d" % s], s0=520 * s + 4 - b)
+        for b in range(4):
+            quant("cid", 128 * b, 128 * b + 128, "zc", ("cid", b), zz + ["zc4"], s0=2084 - b)
+        ts(T.mk16[:], T.it16[:], col(1), A.is_equal, ["it16", "cf"], ["mk16"])
+        ts(T.mk4[:], T.it4[:], col(2), A.is_equal, ["it4", "cf"], ["mk4"])
+        ts(kc(1), col(1), 0.0, A.is_equal, ["cf"], ["kc1"], 32.0, A.mult)
+        ts(kc(2), col(1), 1.0, A.is_equal, ["cf"], ["kc2"])
+        tt(kc(3), kc(1), kc(2), A.add, ["kc1", "kc2"], ["kc3"])
+        tt(kc(5), kc(3), col(6), A.mult, ["kc3", "cf"], ["kc5"])
+        tt(kc(4), kc(3), kc(5), A.subtract, ["kc3", "kc5"], ["kc4"])
+        memset(T.kb[:], 0.0, ["kb"])
+        for q in range(8):
+            ts(T.kb[:, 64 * q + q // 2:64 * q + 64:4], T.onesb[:, 0:16], kc(4 + q % 2), A.mult,
+               ["onesb", "kc4", "kc5", "kb"], ["kb%d" % q])
+        quant("ke", 0, 128, "kb", "ke", ["kb"] + ["kb%d" % q for q in range(8)])
+        act(kc(6), col(3), F.Copy, ["cf"], ["kc6"], scale=1024.0)
+        act(kc(7), col(3), F.Copy, ["cf"], ["kc7"], scale=512.0)
+        act(kc(8), col(4), F.Copy, ["cf"], ["kc8"], scale=8.0, bias=-208.0)
+        act(kc(9), kc(8), F.Copy, ["kc8"], ["kc9"], scale=-1.0, bias=6128.0)
+        act(kc(10), col(5), F.Identity, ["kc8", "kc9", "cf"], ["kc10"], scale=kc(9), bias=kc(8))
+        act(kc(11), col(5), F.Copy, ["cf"], ["kc11"], scale=-33.0, bias=1.0)
+        act(kc(12), col(4), F.Copy, ["cf"], ["kc12"], scale=256.0)
+        act(T.itb[:], T.itb[:], F.Identity, ["itb", "kc12"], ["itb"], bias=kc(12))
+        ts(T.il3[:], T.il2[:], col(1), A.add, ["il2", "cf"], ["il3"])
+        vcopy(T.wlist[:], T.il3[:], ["il3"], ["wlist"])
+        for t in (1, 2):
+            dmas("Y", [(cv("qx%d" % t, a, a + 256), cv("qx0", a, a + 256)) for a in (0, 512)] +
+                 [(T["qx%d_s" % t][:, a:a + 256], T.qx0_s[:, a:a + 256]) for a in (0, 512)], ["z0", "z0b"], ["z%d" % t])
+
+    def wrap(src, mk, rs, srckeys):
+        tt(T.msk[:], src, T[mk][:], A.mult, srckeys + [mk], ["msk"])
+        op("V", V.tensor_tensor_scan, (T.scn[:], T[rs][:], T.msk[:], 0.0, A.mult, A.add), [rs, "msk"], ["scn"])
+
+    for t in range(R):
+        qx = "qx%d" % t
+        X = ("qx", t)
+        zk = ["z0", "z0b"] if t == 0 else ["z%d" % t]
+        remote(cv("land%d" % t, 0, 256), cv(qx, 256, 512), "arr%d" % t, [X])
+        remote(T["land%d_s" % t][:], T[qx + "_s"][:, 256:512], "arr%d" % t, [X])
+        iota("ww", [[0, 1024]], 0, 0)
+        land, lin = "land%d" % t, "lin%d" % t
+        lastw[land] = ("arr%d" % t, 2 * n_in)
+        lastw[lin] = ("lst%d" % t, n_in)
+        total["arr%d" % t] = 2 * n_in
+        total["lst%d" % t] = n_in
+
+        for b in range(2):
+            mm((4, 7)[b], 128, qx, 256 + 128 * b, "qu", 0, True, True, [X, "qu"])
+
+        def rows(h, banks=(0, 1)):
+            for i in banks:
+                for j in range(2):
+                    gr = 4 * h + 2 * i + j
+                    mm(2 * h + i, 512, "qr", 128 * gr, qx, 256 - 256 * j, j == 0, j == 1, [X] + zk + qrk(0, gr))
+        rows(0, (0,))
+        for b in range(2):
+            vcopy(T.cols[:, 128 * b:128 * b + 128], bank((4, 7)[b], 128), [("K", (4, 7)[b])], [("cols", b)])
+        quant("qn", 0, 256, "xn", "qn", ["xn"] if t == 0 else [("xn", 0), ("xn", 1)])
+        flip = {"V": 0, "S": 0}
+
+        def diff(e, s, gr, b, lo):
+            k = {"V": (5, 6), "S": (7, 4)}[e][flip[e] % 2]
+            flip[e] += 1
+            a = 128 * (8 * s + gr)
+            mm(k, 128, "qr", a, "qn", lo, True, False, qrk(s, gr) + ["qn"])
+            mm(k, 128, qx, 256 + 128 * b, "qr", a, False, True, qrk(s, gr) + [X])
+            return k
+
+        pairs = [(gr, b) for gr in range(8) for b in range(2)]
+        same, other = list(pairs), list(pairs)
+        s2k = [("m2", gr, b, i) for gr, b in pairs for i in range(2)]
+
+        def s2_same(n):
+            for gr, b in same[:n]:
+                k = diff("V", 1, gr, b, 128 * b)
+                o = 1024 * (gr // 2) + 512 * b
+                tt(T.m2[:, o + 2 * (gr % 2):o + 512:4], bank(k, 128), T["thr%d" % b][:, 128 * b:128 * b + 128], A.is_gt,
+                   [("K", k), "thr%d" % b], [("m2", gr, b, 0)])
+            del same[:n]
+
+        def s2_other(n):
+            for gr, b in other[:n]:
+                k = diff("S", 1, gr, b, 128 - 128 * b)
+                o = 1024 * (gr // 2) + 512 - 512 * b
+                act(T.m2[:, o + 2 * (gr % 2) + 1:o + 512:4], bank(k, 128), F.Sign, [("K", k)], [("m2", gr, b, 1)],
+                    bias=(1 - 2 * b) * 2.0 ** -120)
+            del other[:n]
+
+        def sign(h, k):
+            c = 128 * (k % 2) + 16 * (4 * h + k // 2)
+            for a, n in ((0, 1), (1, 1)) if h + k == 0 else ((0, 2),):
+                act(T.dd[:, 1024 * k + 512 * a:1024 * k + 512 * (a + n)], T["pr%d" % h][:, 512 * a:512 * (a + n)], F.Sign,
+                    [("K", 2 * h + i) for i in range(a, a + n)] + [("cols", k % 2)], [("dd", k, i) for i in range(a, a + n)],
+                    scale=-1.0, bias=T.cols[:, c:c + 1])
+
+        def fix(h, k):
+            b, tq, base, dg = k % 2, k % 4, 4096 * (k // 4), 128 * k
+            dk = [("dd", k, 0), ("dd", k, 1)]
+            if dg:
+                ts(T.mt[:, base + tq:base + 4 * dg:4], T.dd[:, 1024 * k:1024 * k + dg], 0.0, A.is_gt, dk, [("mt", k, 0)])
+            if dg + 128 < 1024:
+                ts(T.mt[:, base + 4 * (dg + 128) + tq:base + 4096:4], T.dd[:, 1024 * k + dg + 128:1024 * k + 1024], 0.0, A.is_ge, dk, [("mt", k, 1)])
+            kk = diff("V", 0, 4 * h + k // 2, b, 128 * b)
+            tt(T.mt[:, base + 4 * dg + tq:base + 4 * (dg + 128):4], bank(kk, 128), T["thr%d" % b][:, 128 * b:128 * b + 128], A.is_gt,
+               [("K", kk), "thr%d" % b], [("mt", k, 2)])
+
+        def qm(h, i):
+            m0 = 1024 * (2 * h + i)
+            for a in (0, 512):
+                quant("mq", m0 + a, m0 + a + 512, "mt", ("mq", h, i, a), [("mt", k, e) for k in range(4 * i, 4 * i + 4) for e in range(3)],
+                      s0=4096 * i + 4 * a)
+
+        def count(h, i, gis, first=False, last=False):
+            m0 = 1024 * (2 * h + i)
+            for gi in gis:
+                gr = 4 * h + gi
+                mk = [("mq", h, i, 512 * (gi // 2)), "cc0", "cc1"]
+                if gi // 2 == i:
+                    mm(1, 256, "cc", 256 * (1 + gi % 2) + 112 - 16 * gr, "mq", m0 + 256 * gi, first and gi % 2 == 0, last and gi % 2 == 1, mk)
+            for gi in gis:
+                gr = 4 * h + gi
+                mk = [("mq", h, i, 512 * (gi // 2)), "cc0", "cc1"]
+                mm(0, 256, "cc", 112 - 16 * gr, "mq", m0 + 256 * gi, first and gi == 0, last and gi == 3, mk)
+
+        s2_same(1)
+        rows(0, (1,))
+        s2_same(1)
+        for k in range(8):
+            sign(0, k)
+            s2_other(1)
+            if k == 0:
+                rows(1)
+            s2_same(2)
+            fix(0, k)
+            if k % 4 == 3:
+                qm(0, k // 4)
+        if t == 0:
+            setup_late()
+        for k in range(8):
+            sign(1, k)
+            s2_other(2)
+            fix(1, k)
+            if k == 1:
+                count(0, 0, range(4), True)
+                count(0, 1, range(4))
+            if k == 3:
+                qm(1, 0)
+                for a in (0, 512):
+                    quant("m2q", a, a + 512, "m2", ("m2q", a), s2k, s0=4 * a)
+            if k == 4:
+                for q in range(4):
+                    mm(4, 256, "cc", 768 + 112 - 32 * q, "m2q", 256 * q, q == 0, q == 3, [("m2q", 512 * (q // 2)), "cc1"])
+            if k == 5:
+                wrap(bank(4, 256), "mk16", "rs16", [("K", 4)])
+                ts(T.n2l[:], T.scn[:, 15:256:16], 64.0, A.add, ["scn"], ["n2l"])
+                vcopy(T.leaf[:, 0:256].indirect(T.n2l[:, 0:16]), T.itb[:], ["itb", "n2l"], ["leaf"])
+                dmas("Y", [(T.ld[16 * (q // 4):16 * (q // 4) + 16, 256 * (q % 4):256 * (q % 4) + 256], T.leaf[16 * q:16 * q + 16, :]) for q in range(8)], ["leaf"], ["ld"])
+                dmas("Y", [(T.lw[16 * q:16 * q + 16, :], T.ld[16 * (q % 2):16 * (q % 2) + 16, :]) for q in range(8)], ["ld"], ["lw"])
+                count(1, 0, range(4))
+        qm(1, 1)
+
+        wins = [(s, b) for s in range(4) for b in range(4)] + [(4, b) for b in range(4)]
+        wn = [0]
+        pend = []
+
+        def win_mm(n):
+            for _i in range(n):
+                if wins:
+                    s, b = wins.pop(0)
+                    k = (7, 2, 3, 5, 6)[wn[0] % 5]
+                    wn[0] += 1
+                    if s < 4:
+                        mm(k, 256, "cwn", 128 * (4 * s + b), land, 0, True, True, [land, ("cwn", s, b)])
+                    else:
+                        mm(k, 256, "cid", 128 * b, qx, 256, True, True, [X, ("cid", b)])
+                    pend.append((k, s, b))
+
+        def win_cp(n):
+            for _i in range(n):
+                if pend:
+                    k, s, b = pend.pop(0)
+                    if s < 4:
+                        o = 1024 * b + 256 * s
+                        act(T.win[:, o:o + 256], bank(k, 256), F.Copy, [("K", k)], [("win", s, b)])
+                    else:
+                        act(T.fx[:, b:1024:4], bank(k, 256), F.Copy, [("K", k)], [("fx", b)])
+        win_mm(2)
+        count(1, 1, (0, 1))
+        win_mm(3)
+        win_cp(4)
+        count(1, 1, (2, 3), last=True)
+
+        act(T.ab[:], bank(1, 256), F.Copy, [("K", 1)], ["ab"], scale=0.03125, bias=191.515625)
+        act(T.da[:], T.ab[:], F.Identity, ["ab", "kc10", "kc11"], ["da"], scale=kc(11), bias=kc(10))
+        act(T.dn[:], bank(1, 256), F.Copy, [("K", 1), "cf"], ["dn"], scale=col(5))
+        wrap(bank(0, 256), "mk16", "rs16", [("K", 0)])
+        vcopy(T.pl[:], T.scn[:, 15:256:16], ["scn"], ["pl"])
+        tt(T.dat[:], T.dn[:], T.da[:], A.add, ["dn", "da"], ["dat"])
+        vcopy(T.ww[:, 0:1024].indirect(T.pl[:, 0:16]), T.dat[:], ["pl", "dat"], ["ww"])
+        quant("qw", 0, 256, "ww", "qw", ["ww"])
+        win_cp(1)
+        win_mm(4)
+        mm(4, 256, "ke", 0, "qw", 0, True, True, ["ke", "qw"])
+        win_cp(4)
+        while wins or pend:
+            win_mm(3)
+            win_cp(3)
+        wrap(bank(4, 256), "mk16", "rs16", [("K", 4)])
+        ts(T.ql[:], T.scn[:, 15:256:16], 528.0, A.add, ["scn"], ["ql"])
+        wrap(T.lw[:, 0:1024].indirect(T.ql[:, 0:16]), "mk4", "rs4", ["lw", "ql"])
+        el = "el%d" % t
+        ts(T[el][:], T.scn[:, 3:256:4], kc(6), A.add, ["scn", "kc6"], [el])
+        remote(T[lin][:], T[el][:], "lst%d" % t, [el])
+
+        wrap(bank(1, 256), "mk16", "rs16", [("K", 1)])
+        vcopy(T.n1l[:], T.scn[:, 15:256:16], ["scn"], ["n1l"])
+        vcopy(T.psb[:], bank(0, 256), [("K", 0)], ["psb"])
+        vcopy(T.awin[:, 0:256].indirect(T.n1l[:, 0:16]), T.psb[:], ["n1l", "psb"], ["awin"])
+        wrap(T.awin[:, 0:256].indirect(T.n2l[:, 0:16]), "mk4", "rs4", ["awin", "n2l"])
+        vcopy(T.xi[:], T.scn[:, 3:256:4], ["scn"], ["xi"])
+        ts(T.xi2[:], T.xi[:], 2, A.logical_shift_right, ["xi"], ["xi2"], 127, A.bitwise_and)
+        ts(T.xi3[:], T.xi[:], 3, A.bitwise_and, ["xi"], ["xi3"])
+        ts(T.xi3[:], T.xi3[:], 128.0, A.mult, ["xi3", "kc7"], ["xi3"], kc(7), A.add)
+        tt(T.xi2[:], T.xi2[:], T.xi3[:], A.add, ["xi2", "xi3"], ["xi2"])
+        vcopy(T.xl[:], T.xi2[:], ["xi2"], ["xl"])
+        if t == R - 1:
+            vcopy(T.dfull[:], T.awin[:, 0:256].indirect(T.n2l[:, 0:16]), ["awin", "n2l"], ["dfull"])
+            ts(T.dfull[:], T.dfull[:], 2.0, A.mult, ["dfull", "cf"], ["dfull"], col(6), A.add)
+            dmas("Y", [(T.op[q:q + 1, :], T.dfull[16 * q:16 * q + 1, :]) for q in range(8)], ["dfull"], ["op"])
+            quant("qv", 0, 128, "vb", "qv", ["vb"])
+        if t == 0:
+            vcopy(T.qwr[:].bitcast(dt.uint32), T.wq[:, 0:512].bitcast(dt.uint32).indirect(T.wlist[:, 0:128]), ["wq", "wlist"], ["qwr"])
+            act(T.qwr_s[:], T.wq_s[:, 0:512].indirect(T.wlist[:, 0:128]), F.Copy, ["wqs", "wlist"], ["qwrs"])
+
+        wk = [("win", s, b) for s in range(4) for b in range(4)] + [lin]
+        for i in range(2):
+            act(T.etmp[:, 256 * i:256 * i + 256], T.win[:, 0:4096].indirect(T[lin][:, 16 * i:16 * i + 16]), F.Copy, wk, [("etmp", i)])
+            tt(T.eb[:, 256 * i:256 * i + 256], T.win[:, 0:4096].indirect(T[lin][:, 32 + 16 * i:48 + 16 * i]), T.etmp[:, 256 * i:256 * i + 256], A.add,
+               wk + [("etmp", i)], [("eb", i)])
+        quant("qe", 0, 128, "eb", "qe", [("eb", 0), ("eb", 1)])
+        for i in range(16):
+            k, s, b = i % 8, i // 4, i % 4
+            mm(k, 128, "qwr", 128 * (4 * b + s), "qe", 0, True, True, ["qwr", "qwrs", "qe"])
+            o = 512 * b + 128 * s
+            if i % 2:
+                ts(T.winh[:, o:o + 128], bank(k, 128), 0.015625, A.mult, [("K", k)], [("winh", i)])
+            else:
+                act(T.winh[:, o:o + 128], bank(k, 128), F.Copy, [("K", k)], [("winh", i)], scale=0.015625)
+        hk = [("winh", i) for i in range(16)] + ["xl"] + [("fx", b) for b in range(4)]
+        for i in range(2):
+            c = 512 * i
+            tt(T.xs[:, c:c + 512], T.winh[:, 0:2048].indirect(T.xl[:, 32 * i:32 * i + 32]), T.fx[:, c:c + 512], A.add, hk, [("xs", i)])
+            if t < R - 1:
+                act(T.xn[:, c:c + 512], T.xs[:, c:c + 512], F.Copy, [("xs", i)], [("xn", i), "xn"] if t == 0 else [("xn", i)], scale=-1.0)
+        if t < R - 1:
+            quant("qx%d" % (t + 1), 256, 512, "xs", ("qx", t + 1), [("xs", 0), ("xs", 1)])
+        else:
+            quant("qx3", 0, 256, "xs", "qx3", [("xs", 0), ("xs", 1)])
+
+    mm(0, 256, "qv", 0, "qx3", 0, True, True, ["qv", "qx3"])
+    dmas("Y", [(T.oc[:, :], cv("qx3", 0, 256))], ["qx3"], ["oc"])
+    dmas("S", [(T.osc[4 * k:4 * k + 4, :], T.qx3_s[32 * k:32 * k + 4, 0:256]) for k in range(4)], ["qx3"], ["osc"])
+    vcopy(T.ysb[:], bank(0, 256), [("K", 0)], ["ysb"])
+    dmas("Y", [(T.y[:, :], T.ysb[:])], ["ysb"], ["y"])
+    total["ls"] = nrem[0] * n_eng
+    for e in cnt:
+        total["s" + e] = cnt[e]
+    for s in sorted(total):
+        g.wait_ge(T.sem[s], total[s])

@@ -23,7 +23,7 @@ for _t in range(R):
 for _n, _w in (("qx3", 256), ("qn", 256), ("qu", 128), ("qr", 2048), ("qv", 128), ("wq", 512), ("qwr", 2048), ("cc", 1024),
                ("cid", 512), ("cwn", 2048), ("ke", 128), ("m2q", 1024), ("mq", 4096), ("qw", 256), ("qe", 128)):
     _q(_n, _w)
-for _n, _w in (("xb", 1024), ("xs", 1024), ("xn", 1024), ("ub", 512), ("vb", 512), ("zero", 1024), ("cst", 4096), ("zc", 2600),
+for _n, _w in (("xb", 1024), ("xs", 1024), ("xn", 1024), ("ub", 512), ("vb", 512), ("zero", 1024), ("cst", 3080), ("zc", 2600),
                ("kb", 512), ("onesb", 128), ("halfb", 128), ("negb", 256), ("thr0", 256), ("thr1", 256), ("mt", 8192), ("m2", 4096),
                ("dd", 8192), ("win", 4096), ("winh", 2048), ("fx", 1024), ("etmp", 512), ("eb", 512), ("ww", 1024),
                ("ab", 256), ("da", 256), ("dn", 256), ("dat", 256)):
@@ -42,6 +42,9 @@ _b("pr0", 1024, "float32", "psum")
 _b("pr1", 1024, "float32", "psum")
 for _k in range(4, 8):
     _b("pb%d" % _k, 512, "float32", "psum")
+
+SAME = ((1, 1, 1, 2, 2, 2, 2, 2), (1, 0, 0, 0, 0, 0, 0, 0))
+OTHER = ((0, 1, 1, 1, 2, 2, 2, 2), (3, 2, 0, 0, 0, 0, 0, 0))
 
 
 def rank_program(g, core, T, topo):
@@ -184,14 +187,6 @@ def rank_program(g, core, T, topo):
     pick_u(0)
     quant("qx0", 256, 512, "xb", ("qx", 0), ["xb"])
     act(T.xn[:], T.xb[:], F.Copy, ["xb"], ["xn"], scale=-1.0)
-    pick_u(1024)
-    pick_u(512)
-    pick_u(1536)
-    for i in range(4):
-        act(T.cst[:, 1024 * i:1024 * i + 1024], T.zero[:], F.Copy, ["zero"], ["cst%d" % (9 + i)])
-    for c, sh, an in ((1, 0, 15), (2, 2, 3), (3, 0, 3), (4, 4, 3), (5, 0, 1), (6, 6, 1)):
-        ts(T.ci[:, c:c + 1], T.ci[:, 0:1], sh, A.logical_shift_right, ["ci"], ["ci%d" % c], an, A.bitwise_and)
-    vcopy(T.cf[:, 0:7], T.ci[:, 0:7], ["ci"] + ["ci%d" % c for c in range(1, 7)], ["cf"])
 
     def col(c):
         return T.cf[:, c:c + 1]
@@ -203,7 +198,12 @@ def rank_program(g, core, T, topo):
         i = (8 * s + gr) // 4
         return [("qr", i), ("qrs", i)]
 
-    def setup_late():
+    def setup_cols():
+        for c, sh, an in ((1, 0, 15), (2, 2, 3), (3, 0, 3), (4, 4, 3), (5, 0, 1), (6, 6, 1)):
+            ts(T.ci[:, c:c + 1], T.ci[:, 0:1], sh, A.logical_shift_right, ["ci"], ["ci%d" % c], an, A.bitwise_and)
+        vcopy(T.cf[:, 0:7], T.ci[:, 0:7], ["ci"] + ["ci%d" % c for c in range(1, 7)], ["cf"])
+
+    def setup_pool():
         iota("it16", [[0, 16], [1, 16]], 0, 0)
         iota("it4", [[0, 64], [1, 4]], 0, 0)
         for nm, q in (("rs16", 16), ("rs4", 4)):
@@ -211,20 +211,29 @@ def rank_program(g, core, T, topo):
             select(T[nm][:], T[nm][:], [[0, 256 // q], [1, q]], A.not_equal, 0, 0, [nm], [nm])
         iota("itb", [[1, 256]], 0, 0)
         iota("il2", [[32, 16], [16, 2], [0, 4]], 0, 0)
-        memset(T.cst[:, 448:512], 1.0, ["cst8"], ["cst9"])
-        for t in range(4):
-            o = 1024 * (1 + t // 2) + 448
-            memset(T.cst[:, o + t:o + 64:4], 1.0, ["cst%d" % t], ["cst10", "cst11"])
-            o = 3072 + 448 + 64 * (t // 2)
-            memset(T.cst[:, o + t:o + 64:4], 1.0 - 0.5 * (t % 2), ["cst%d" % (4 + t)], ["cst12"])
-        for i in range(2):
-            quant("cc", 512 * i, 512 * i + 512, "cst", "cc%d" % i, ["cst%d" % t for t in range(13)], s0=2048 * i)
-        for s in range(4):
+
+    def setup_windows(ss):
+        for s in ss:
             for b in range(4):
                 a = 128 * (4 * s + b)
                 quant("cwn", a, a + 128, "zc", ("cwn", s, b), zz + ["zc%d" % s], s0=520 * s + 4 - b)
+
+    def setup_own():
         for b in range(4):
             quant("cid", 128 * b, 128 * b + 128, "zc", ("cid", b), zz + ["zc4"], s0=2084 - b)
+
+    def setup_ones():
+        memset(T.cst[:], 0.0, ["cst"])
+        memset(T.cst[:, 448:512], 1.0, ["cst8"], ["cst"])
+        for t in range(4):
+            if t < 2:
+                memset(T.cst[:, 1476 + t:1540:4], 1.0, ["cst%d" % t], ["cst"])
+            o = 2504 + 64 * (t // 2)
+            memset(T.cst[:, o + t:o + 64:4], 1.0 - 0.5 * (t % 2), ["cst%d" % (4 + t)], ["cst"])
+        for i, o in enumerate((0, 1028, 1026, 2056)):
+            quant("cc", 256 * i, 256 * i + 256, "cst", "cc%d" % (i // 2), ["cst", "cst0", "cst1", "cst4", "cst5", "cst6", "cst7", "cst8"], s0=o)
+
+    def setup_lists():
         ts(T.mk16[:], T.it16[:], col(1), A.is_equal, ["it16", "cf"], ["mk16"])
         ts(T.mk4[:], T.it4[:], col(2), A.is_equal, ["it4", "cf"], ["mk4"])
         ts(kc(1), col(1), 0.0, A.is_equal, ["cf"], ["kc1"], 32.0, A.mult)
@@ -271,12 +280,11 @@ def rank_program(g, core, T, topo):
         for b in range(2):
             mm((4, 7)[b], 128, qx, 256 + 128 * b, "qu", 0, True, True, [X, "qu"])
 
-        def rows(h, banks=(0, 1)):
-            for i in banks:
-                for j in range(2):
-                    gr = 4 * h + 2 * i + j
-                    mm(2 * h + i, 512, "qr", 128 * gr, qx, 256 - 256 * j, j == 0, j == 1, [X] + zk + qrk(0, gr))
-        rows(0, (0,))
+        def rows(h, i):
+            for j in range(2):
+                gr = 4 * h + 2 * i + j
+                mm(2 * h + i, 512, "qr", 128 * gr, qx, 256 - 256 * j, j == 0, j == 1, [X] + zk + qrk(0, gr))
+        rows(0, 0)
         for b in range(2):
             vcopy(T.cols[:, 128 * b:128 * b + 128], bank((4, 7)[b], 128), [("K", (4, 7)[b])], [("cols", b)])
         quant("qn", 0, 256, "xn", "qn", ["xn"] if t == 0 else [("xn", 0), ("xn", 1)])
@@ -346,43 +354,6 @@ def rank_program(g, core, T, topo):
                 mk = [("mq", h, i, 512 * (gi // 2)), "cc0", "cc1"]
                 mm(0, 256, "cc", 112 - 16 * gr, "mq", m0 + 256 * gi, first and gi == 0, last and gi == 3, mk)
 
-        s2_same(1)
-        rows(0, (1,))
-        s2_same(1)
-        for k in range(8):
-            sign(0, k)
-            s2_other(1)
-            if k == 0:
-                rows(1)
-            s2_same(2)
-            fix(0, k)
-            if k % 4 == 3:
-                qm(0, k // 4)
-        if t == 0:
-            setup_late()
-        for k in range(8):
-            sign(1, k)
-            s2_other(2)
-            fix(1, k)
-            if k == 1:
-                count(0, 0, range(4), True)
-                count(0, 1, range(4))
-            if k == 3:
-                qm(1, 0)
-                for a in (0, 512):
-                    quant("m2q", a, a + 512, "m2", ("m2q", a), s2k, s0=4 * a)
-            if k == 4:
-                for q in range(4):
-                    mm(4, 256, "cc", 768 + 112 - 32 * q, "m2q", 256 * q, q == 0, q == 3, [("m2q", 512 * (q // 2)), "cc1"])
-            if k == 5:
-                wrap(bank(4, 256), "mk16", "rs16", [("K", 4)])
-                ts(T.n2l[:], T.scn[:, 15:256:16], 64.0, A.add, ["scn"], ["n2l"])
-                vcopy(T.leaf[:, 0:256].indirect(T.n2l[:, 0:16]), T.itb[:], ["itb", "n2l"], ["leaf"])
-                dmas("Y", [(T.ld[16 * (q // 4):16 * (q // 4) + 16, 256 * (q % 4):256 * (q % 4) + 256], T.leaf[16 * q:16 * q + 16, :]) for q in range(8)], ["leaf"], ["ld"])
-                dmas("Y", [(T.lw[16 * q:16 * q + 16, :], T.ld[16 * (q % 2):16 * (q % 2) + 16, :]) for q in range(8)], ["ld"], ["lw"])
-                count(1, 0, range(4))
-        qm(1, 1)
-
         wins = [(s, b) for s in range(4) for b in range(4)] + [(4, b) for b in range(4)]
         wn = [0]
         pend = []
@@ -408,10 +379,62 @@ def rank_program(g, core, T, topo):
                         act(T.win[:, o:o + 256], bank(k, 256), F.Copy, [("K", k)], [("win", s, b)])
                     else:
                         act(T.fx[:, b:1024:4], bank(k, 256), F.Copy, [("K", k)], [("fx", b)])
-        win_mm(2)
-        count(1, 1, (0, 1))
+
+        if t == 0:
+            rows(0, 1)
+            sign(0, 0)
+            pick_u(1024)
+            s2_same(2)
+            setup_cols()
+            setup_windows((0, 1))
+            setup_pool()
+        else:
+            s2_same(1)
+            rows(0, 1)
+            s2_same(1)
+        for k in range(8):
+            if t or k:
+                sign(0, k)
+            if t == 0 and k in (1, 2):
+                pick_u(1024 * k - 512)
+            s2_other(OTHER[0][k])
+            if k in (2, 4):
+                rows(1, k // 2 - 1)
+            s2_same(SAME[0][k])
+            fix(0, k)
+            if t == 0 and 2 < k < 7:
+                (setup_ones, lambda: setup_windows((2,)), lambda: setup_windows((3,)), setup_own)[k - 3]()
+            if k % 4 == 3:
+                qm(0, k // 4)
+        if t == 0:
+            setup_lists()
+        for k in range(8):
+            sign(1, k)
+            s2_other(OTHER[1][k])
+            s2_same(SAME[1][k])
+            fix(1, k)
+            if k == 1:
+                for a in (0, 512):
+                    quant("m2q", a, a + 512, "m2", ("m2q", a), s2k, s0=4 * a)
+            if k == 2:
+                for q in range(4):
+                    mm(4, 256, "cc", 768 + 112 - 32 * q, "m2q", 256 * q, q == 0, q == 3, [("m2q", 512 * (q // 2)), "cc1"])
+            if k == 3:
+                count(0, 0, range(4), True)
+                qm(1, 0)
+                wrap(bank(4, 256), "mk16", "rs16", [("K", 4)])
+                ts(T.n2l[:], T.scn[:, 15:256:16], 64.0, A.add, ["scn"], ["n2l"])
+                vcopy(T.leaf[:, 0:256].indirect(T.n2l[:, 0:16]), T.itb[:], ["itb", "n2l"], ["leaf"])
+                dmas("Y", [(T.ld[16 * (q // 4):16 * (q // 4) + 16, 256 * (q % 4):256 * (q % 4) + 256], T.leaf[16 * q:16 * q + 16, :]) for q in range(8)], ["leaf"], ["ld"])
+                dmas("Y", [(T.lw[16 * q:16 * q + 16, :], T.ld[16 * (q % 2):16 * (q % 2) + 16, :]) for q in range(8)], ["ld"], ["lw"])
+            if k == 4:
+                count(0, 1, range(4))
+            if k == 5:
+                count(1, 0, range(4))
+        qm(1, 1)
         win_mm(3)
-        win_cp(4)
+        count(1, 1, (0, 1))
+        win_cp(3)
         count(1, 1, (2, 3), last=True)
 
         act(T.ab[:], bank(1, 256), F.Copy, [("K", 1)], ["ab"], scale=0.03125, bias=191.515625)
@@ -422,10 +445,9 @@ def rank_program(g, core, T, topo):
         tt(T.dat[:], T.dn[:], T.da[:], A.add, ["dn", "da"], ["dat"])
         vcopy(T.ww[:, 0:1024].indirect(T.pl[:, 0:16]), T.dat[:], ["pl", "dat"], ["ww"])
         quant("qw", 0, 256, "ww", "qw", ["ww"])
-        win_cp(1)
-        win_mm(4)
+        win_mm(5)
         mm(4, 256, "ke", 0, "qw", 0, True, True, ["ke", "qw"])
-        win_cp(4)
+        win_cp(5)
         while wins or pend:
             win_mm(3)
             win_cp(3)
@@ -441,12 +463,6 @@ def rank_program(g, core, T, topo):
         vcopy(T.psb[:], bank(0, 256), [("K", 0)], ["psb"])
         vcopy(T.awin[:, 0:256].indirect(T.n1l[:, 0:16]), T.psb[:], ["n1l", "psb"], ["awin"])
         wrap(T.awin[:, 0:256].indirect(T.n2l[:, 0:16]), "mk4", "rs4", ["awin", "n2l"])
-        vcopy(T.xi[:], T.scn[:, 3:256:4], ["scn"], ["xi"])
-        ts(T.xi2[:], T.xi[:], 2, A.logical_shift_right, ["xi"], ["xi2"], 127, A.bitwise_and)
-        ts(T.xi3[:], T.xi[:], 3, A.bitwise_and, ["xi"], ["xi3"])
-        ts(T.xi3[:], T.xi3[:], 128.0, A.mult, ["xi3", "kc7"], ["xi3"], kc(7), A.add)
-        tt(T.xi2[:], T.xi2[:], T.xi3[:], A.add, ["xi2", "xi3"], ["xi2"])
-        vcopy(T.xl[:], T.xi2[:], ["xi2"], ["xl"])
         if t == R - 1:
             vcopy(T.dfull[:], T.awin[:, 0:256].indirect(T.n2l[:, 0:16]), ["awin", "n2l"], ["dfull"])
             ts(T.dfull[:], T.dfull[:], 2.0, A.mult, ["dfull", "cf"], ["dfull"], col(6), A.add)
@@ -462,6 +478,12 @@ def rank_program(g, core, T, topo):
             tt(T.eb[:, 256 * i:256 * i + 256], T.win[:, 0:4096].indirect(T[lin][:, 32 + 16 * i:48 + 16 * i]), T.etmp[:, 256 * i:256 * i + 256], A.add,
                wk + [("etmp", i)], [("eb", i)])
         quant("qe", 0, 128, "eb", "qe", [("eb", 0), ("eb", 1)])
+        vcopy(T.xi[:], T.scn[:, 3:256:4], ["scn"], ["xi"])
+        ts(T.xi2[:], T.xi[:], 2, A.logical_shift_right, ["xi"], ["xi2"], 127, A.bitwise_and)
+        ts(T.xi3[:], T.xi[:], 3, A.bitwise_and, ["xi"], ["xi3"])
+        ts(T.xi3[:], T.xi3[:], 128.0, A.mult, ["xi3", "kc7"], ["xi3"], kc(7), A.add)
+        tt(T.xi2[:], T.xi2[:], T.xi3[:], A.add, ["xi2", "xi3"], ["xi2"])
+        vcopy(T.xl[:], T.xi2[:], ["xi2"], ["xl"])
         for i in range(16):
             k, s, b = i % 8, i // 4, i % 4
             mm(k, 128, "qwr", 128 * (4 * b + s), "qe", 0, True, True, ["qwr", "qwrs", "qe"])

from concourse.mybir import dt, AluOpType as A, ActivationFunctionType as F
import comms_topo

R = 3
SCRATCH = {}
SEMAPHORES = ["sV", "sS", "sP", "sG", "ls"] + ["arr%d" % t for t in range(R)] + ["lst%d" % t for t in range(R)] + ["d%d" % i for i in range(40)]


def _b(name, n, d, where="sbuf"):
    SCRATCH[name] = (where, [128, n], d)


def _q(name, n):
    _b(name, n, "float8_e4m3fn_x4")
    _b(name + "_s", n, "uint8")


for _t in range(R):
    _q("qx%d" % _t, 768)
    _q("land%d" % _t, 256)
    _b("lin%d" % _t, 64, "uint16")
    _b("el%d" % _t, 64, "uint16")
for _n, _w in (("qx3", 256), ("qn", 256), ("qu", 128), ("qr", 2048), ("qv", 128), ("wq", 512), ("qwr", 2048), ("cc", 1024),
               ("cid", 512), ("cwn", 2048), ("ke", 128), ("m2q", 1024), ("mq", 4096), ("qw", 256), ("qe", 128)):
    _q(_n, _w)
for _n, _w in (("xb", 1024), ("xs", 1024), ("xn", 1024), ("ub", 512), ("vb", 512), ("zero", 1024), ("cst", 3080), ("zc", 2600),
               ("kb", 512), ("onesb", 128), ("halfb", 128), ("negb", 256), ("thr0", 256), ("thr1", 256), ("mt", 8192), ("m2", 4096),
               ("dd", 8192), ("win", 4096), ("winh", 2048), ("fx", 1024), ("etmp", 512), ("eb", 512), ("ww", 1024),
               ("ab", 256), ("da", 256), ("dn", 256), ("dat", 256)):
    _b(_n, _w, "bfloat16")
for _n in ("mk16", "rs16", "mk4", "rs4", "msk", "scn", "psb", "awin", "it16", "it4", "dfull", "ysb", "cols", "itb", "leaf"):
    _b(_n, 256, "float32")
_b("lw", 1024, "float32")
_b("cf", 8, "float32")
_b("kc", 16, "float32")
for _n, _w in (("ci", 8), ("il", 128), ("il2", 128), ("il3", 128), ("xi", 64), ("xi2", 64), ("xi3", 64)):
    _b(_n, _w, "int32")
for _n, _w in (("ulist", 128), ("wlist", 128), ("n1l", 16), ("n2l", 16), ("pl", 16), ("ql", 16), ("xl", 64)):
    _b(_n, _w, "uint16")
SCRATCH["ld"] = ("dram", [32, 1024], "float32")
_b("pr0", 1024, "float32", "psum")
_b("pr1", 1024, "float32", "psum")
for _k in range(4, 8):
    _b("pb%d" % _k, 512, "float32", "psum")

SAME = ((1, 1, 1, 2, 2, 2, 2, 2), (1, 0, 0, 0, 0, 0, 0, 0))
OTHER = ((0, 1, 1, 1, 2, 2, 2, 2), (3, 2, 0, 0, 0, 0, 0, 0))


def rank_program(g, core, T, topo):
    rank = T.rank_of(core)
    if rank is None:
        return
    nxt = T.cores[(rank + 1) % len(T.cores)]
    prv = T.cores[(rank - 1) % len(T.cores)]
    rid, pid, _se = topo.addr(nxt)
    mask = topo.mask(core, nxt)
    n_eng = len(topo.engines(core, nxt))
    n_in = len(topo.engines(prv, core))

    eng = {"V": g.vector, "S": g.scalar, "P": g.tensor, "G": g, "Y": g.sync}
    cnt = {"V": 0, "S": 0, "P": 0, "G": 0}
    waited = {e: {} for e in eng}
    lastw, readers, total = {}, {}, {}
    ndma, nrem = [0], [0]

    def need(e, reads, writes, acc=False):
        w = {}
        own = "s" + e

        def add(sv):
            if w.get(sv[0], 0) < sv[1]:
                w[sv[0]] = sv[1]
        for k in reads:
            if k in lastw:
                add(lastw[k])
            if k[0] == "K":
                for sv in readers.get(k, ()):
                    if sv[0] != own:
                        add(sv)
        for k in writes:
            if k in lastw and not (acc and lastw[k][0] == own):
                add(lastw[k])
            for sv in readers.get(k, ()):
                if sv[0] != own:
                    add(sv)
        for s, v in w.items():
            if waited[e].get(s, 0) < v:
                eng[e].wait_ge(T.sem[s], v)
                waited[e][s] = v

    def note(sv, reads, writes):
        for k in reads:
            readers.setdefault(k, []).append(sv)
        for k in writes:
            lastw[k] = sv
            readers[k] = []
        total[sv[0]] = max(total.get(sv[0], 0), sv[1])

    def op(e, fn, args, reads, writes, acc=False, **kw):
        need(e, reads, writes, acc)
        cnt[e] += 1
        fn(*args, **kw).then_inc(T.sem["s" + e], 1)
        note(("s" + e, cnt[e]), reads, writes)

    def dmas(e, pairs, reads, writes):
        need(e, reads, writes)
        s = "d%d" % ndma[0]
        ndma[0] += 1
        for out, in_ in pairs:
            eng[e].dma_start(out, in_).then_inc(T.sem[s], 16)
        note((s, 16 * len(pairs)), reads, writes)

    def remote(out, in_, sem, reads):
        need("G", reads, [])
        g.remote_dma(out, in_, T.sem[sem], T.sem.ls, pid, rid, mask)
        nrem[0] += 1

    V, S, P = g.vector, g.scalar, g.tensor

    def cv(name, a, b):
        return T[name][:, a:b].bitcast(dt.uint8)

    def quant(name, a, b, src, key, reads, s0=0):
        op("V", V.quantize_mx, (T[name][:, a:b], T[name + "_s"][:, a:b], T[src][:, s0:s0 + 4 * (b - a)]), reads, [key])

    def bank(k, n):
        if k < 4:
            return T["pr%d" % (k // 2)][:, 512 * (k % 2):512 * (k % 2) + n]
        return T["pb%d" % k][:, 0:n]

    def mm(k, n, l, la, r, ra, start, stop, reads):
        op("P", P.matmul_mx, (bank(k, n), T[l][:, la:la + 128], T[l + "_s"][:, la:la + 128],
                              T[r][:, ra:ra + n], T[r + "_s"][:, ra:ra + n], start, stop),
           reads, [("K", k)], acc=not start)

    def ts(out, in0, s1, o0, reads, writes, s2=None, o1=None):
        op("V", V.tensor_scalar, (out, in0, s1, s2, o0) if o1 is None else (out, in0, s1, s2, o0, o1), reads, writes)

    def tt(out, a, b, o, reads, writes):
        op("V", V.tensor_tensor, (out, a, b, o), reads, writes)

    def vcopy(out, in_, reads, writes):
        op("V", V.tensor_copy, (out, in_), reads, writes)

    def act(out, in_, f, reads, writes, **kw):
        op("S", S.activation, (out, in_, f), reads, writes, **kw)

    def memset(ap, c, writes, reads=()):
        op("V", V.memset, (ap, c), list(reads), writes)

    def iota(name, pat, base, cm):
        op("G", g.iota, (T[name][:], pat, base, cm), [], [name], allow_small_or_imprecise_dtypes=True)

    def select(out, in_, pat, cmp, base, cm, reads, writes):
        op("G", g.affine_select, (out, in_, pat, cmp, 0.0, base, cm), reads, writes)

    dmas("S", [(T.ub[:], T.u[:, :])], [], ["ub"])
    dmas("Y", [(T.xb[:], T.x[:, :])], [], ["xb"])
    dmas("Y", [(cv("wq", 0, 512), T.wc[:, :])], [], ["wq"])
    dmas("Y", [(T.wq_s[:], T.ws[:, :])], [], ["wqs"])
    dmas("Y", [(T.vb[:], T.v[:, :])], [], ["vb"])

    iota("il", [[1, 2], [16, 8], [0, 8]], 0, 0)
    iota("ci", [[0, 8]], 0, 1)
    memset(T.zero[:], 0.0, ["zero"])
    memset(T.negb[:], -2.0 ** -120, ["negb"])
    memset(T.onesb[:], 1.0, ["onesb"])
    memset(T.halfb[:], 0.5, ["halfb"])
    vcopy(T.ulist[:], T.il[:], ["il"], ["ulist"])
    for b in range(2):
        select(T["thr%d" % b][:], T.negb[:], [[1, 256]], A.is_ge, -1 - 128 * b, -1, ["negb"], ["thr%d" % b])
    for i in range(3):
        act(T.zc[:, 1024 * i:min(2600, 1024 * i + 1024)], T.zero[:, 0:min(1024, 2600 - 1024 * i)], F.Copy, ["zero"], ["zz%d" % i])
    zz = ["zz0", "zz1", "zz2"]
    select(T.zc[:, 2084:2596:4], T.onesb[:], [[-1, 128]], A.is_equal, 0, 1, ["onesb"] + zz, ["zc4"])
    for s in range(4):
        select(T.zc[:, s * 520 + 4:s * 520 + 516:4], T.halfb[:], [[0, 4], [-64, 2], [-1, 16]], A.is_equal, -16 * s, 1, ["halfb"] + zz, ["zc%d" % s])
    quant("qx0", 0, 256, "zero", "z0", ["zero"])
    quant("qx0", 512, 768, "zero", "z0b", ["zero"])
    quant("qu", 0, 128, "ub", "qu", ["ub"])

    def pick_u(a):
        lst = T.ulist[:, a // 16:a // 16 + 32]
        vcopy(T.qr[:, a:a + 512].bitcast(dt.uint32), T.qu[:, 0:128].bitcast(dt.uint32).indirect(lst), ["qu", "ulist"], [("qr", a // 512)])
        act(T.qr_s[:, a:a + 512], T.qu_s[:, 0:128].indirect(lst), F.Copy, ["qu", "ulist"], [("qrs", a // 512)])
    pick_u(0)
    quant("qx0", 256, 512, "xb", ("qx", 0), ["xb"])
    act(T.xn[:], T.xb[:], F.Copy, ["xb"], ["xn"], scale=-1.0)

    def col(c):
        return T.cf[:, c:c + 1]

    def kc(c):
        return T.kc[:, c:c + 1]

    def qrk(s, gr):
        i = (8 * s + gr) // 4
        return [("qr", i), ("qrs", i)]

    def setup_cols():
        for c, sh, an in ((1, 0, 15), (2, 2, 3), (3, 0, 3), (4, 4, 3), (5, 0, 1), (6, 6, 1)):
            ts(T.ci[:, c:c + 1], T.ci[:, 0:1], sh, A.logical_shift_right, ["ci"], ["ci%d" % c], an, A.bitwise_and)
        vcopy(T.cf[:, 0:7], T.ci[:, 0:7], ["ci"] + ["ci%d" % c for c in range(1, 7)], ["cf"])

    def setup_pool():
        iota("it16", [[0, 16], [1, 16]], 0, 0)
        iota("it4", [[0, 64], [1, 4]], 0, 0)
        for nm, q in (("rs16", 16), ("rs4", 4)):
            iota(nm, [[0, 256]], 1, 0)
            select(T[nm][:], T[nm][:], [[0, 256 // q], [1, q]], A.not_equal, 0, 0, [nm], [nm])
        iota("itb", [[1, 256]], 0, 0)
        iota("il2", [[32, 16], [16, 2], [0, 4]], 0, 0)

    def setup_windows(ss):
        for s in ss:
            for b in range(4):
                a = 128 * (4 * s + b)
                quant("cwn", a, a + 128, "zc", ("cwn", s, b), zz + ["zc%d" % s], s0=520 * s + 4 - b)

    def setup_own():
        for b in range(4):
            quant("cid", 128 * b, 128 * b + 128, "zc", ("cid", b), zz + ["zc4"], s0=2084 - b)

    def setup_ones():
        memset(T.cst[:], 0.0, ["cst"])
        memset(T.cst[:, 448:512], 1.0, ["cst8"], ["cst"])
        for t in range(4):
            if t < 2:
                memset(T.cst[:, 1476 + t:1540:4], 1.0, ["cst%d" % t], ["cst"])
            o = 2504 + 64 * (t // 2)
            memset(T.cst[:, o + t:o + 64:4], 1.0 - 0.5 * (t % 2), ["cst%d" % (4 + t)], ["cst"])
        for i, o in enumerate((0, 1028, 1026, 2056)):
            quant("cc", 256 * i, 256 * i + 256, "cst", "cc%d" % (i // 2), ["cst", "cst0", "cst1", "cst4", "cst5", "cst6", "cst7", "cst8"], s0=o)

    def setup_lists():
        ts(T.mk16[:], T.it16[:], col(1), A.is_equal, ["it16", "cf"], ["mk16"])
        ts(T.mk4[:], T.it4[:], col(2), A.is_equal, ["it4", "cf"], ["mk4"])
        ts(kc(1), col(1), 0.0, A.is_equal, ["cf"], ["kc1"], 32.0, A.mult)
        ts(kc(2), col(1), 1.0, A.is_equal, ["cf"], ["kc2"])
        tt(kc(3), kc(1), kc(2), A.add, ["kc1", "kc2"], ["kc3"])
        tt(kc(5), kc(3), col(6), A.mult, ["kc3", "cf"], ["kc5"])
        tt(kc(4), kc(3), kc(5), A.subtract, ["kc3", "kc5"], ["kc4"])
        memset(T.kb[:], 0.0, ["kb"])
        for q in range(8):
            ts(T.kb[:, 64 * q + q // 2:64 * q + 64:4], T.onesb[:, 0:16], kc(4 + q % 2), A.mult,
               ["onesb", "kc4", "kc5", "kb"], ["kb%d" % q])
        quant("ke", 0, 128, "kb", "ke", ["kb"] + ["kb%d" % q for q in range(8)])
        act(kc(6), col(3), F.Copy, ["cf"], ["kc6"], scale=1024.0)
        act(kc(7), col(3), F.Copy, ["cf"], ["kc7"], scale=512.0)
        act(kc(8), col(4), F.Copy, ["cf"], ["kc8"], scale=8.0, bias=-208.0)
        act(kc(9), kc(8), F.Copy, ["kc8"], ["kc9"], scale=-1.0, bias=6128.0)
        act(kc(10), col(5), F.Identity, ["kc8", "kc9", "cf"], ["kc10"], scale=kc(9), bias=kc(8))
        act(kc(11), col(5), F.Copy, ["cf"], ["kc11"], scale=-33.0, bias=1.0)
        act(kc(12), col(4), F.Copy, ["cf"], ["kc12"], scale=256.0)
        act(T.itb[:], T.itb[:], F.Identity, ["itb", "kc12"], ["itb"], bias=kc(12))
        ts(T.il3[:], T.il2[:], col(1), A.add, ["il2", "cf"], ["il3"])
        vcopy(T.wlist[:], T.il3[:], ["il3"], ["wlist"])
        for t in (1, 2):
            dmas("Y", [(cv("qx%d" % t, a, a + 256), cv("qx0", a, a + 256)) for a in (0, 512)] +
                 [(T["qx%d_s" % t][:, a:a + 256], T.qx0_s[:, a:a + 256]) for a in (0, 512)], ["z0", "z0b"], ["z%d" % t])

    def wrap(src, mk, rs, srckeys):
        tt(T.msk[:], src, T[mk][:], A.mult, srckeys + [mk], ["msk"])
        op("V", V.tensor_tensor_scan, (T.scn[:], T[rs][:], T.msk[:], 0.0, A.mult, A.add), [rs, "msk"], ["scn"])

    for t in range(R):
        qx = "qx%d" % t
        X = ("qx", t)
        zk = ["z0", "z0b"] if t == 0 else ["z%d" % t]
        remote(cv("land%d" % t, 0, 256), cv(qx, 256, 512), "arr%d" % t, [X])
        remote(T["land%d_s" % t][:], T[qx + "_s"][:, 256:512], "arr%d" % t, [X])
        iota("ww", [[0, 1024]], 0, 0)
        land, lin = "land%d" % t, "lin%d" % t
        lastw[land] = ("arr%d" % t, 2 * n_in)
        lastw[lin] = ("lst%d" % t, n_in)
        total["arr%d" % t] = 2 * n_in
        total["lst%d" % t] = n_in

        for b in range(2):
            mm((4, 7)[b], 128, qx, 256 + 128 * b, "qu", 0, True, True, [X, "qu"])

        def rows(h, i):
            for j in range(2):
                gr = 4 * h + 2 * i + j
                mm(2 * h + i, 512, "qr", 128 * gr, qx, 256 - 256 * j, j == 0, j == 1, [X] + zk + qrk(0, gr))
        rows(0, 0)
        for b in range(2):
            vcopy(T.cols[:, 128 * b:128 * b + 128], bank((4, 7)[b], 128), [("K", (4, 7)[b])], [("cols", b)])
        quant("qn", 0, 256, "xn", "qn", ["xn"] if t == 0 else [("xn", 0), ("xn", 1)])
        flip = {"V": 0, "S": 0}

        def diff(e, s, gr, b, lo):
            k = {"V": (5, 6), "S": (7, 4)}[e][flip[e] % 2]
            flip[e] += 1
            a = 128 * (8 * s + gr)
            mm(k, 128, "qr", a, "qn", lo, True, False, qrk(s, gr) + ["qn"])
            mm(k, 128, qx, 256 + 128 * b, "qr", a, False, True, qrk(s, gr) + [X])
            return k

        pairs = [(gr, b) for gr in range(8) for b in range(2)]
        same, other = list(pairs), list(pairs)
        s2k = [("m2", gr, b, i) for gr, b in pairs for i in range(2)]

        def s2_same(n):
            for gr, b in same[:n]:
                k = diff("V", 1, gr, b, 128 * b)
                o = 1024 * (gr // 2) + 512 * b
                tt(T.m2[:, o + 2 * (gr % 2):o + 512:4], bank(k, 128), T["thr%d" % b][:, 128 * b:128 * b + 128], A.is_gt,
                   [("K", k), "thr%d" % b], [("m2", gr, b, 0)])
            del same[:n]

        def s2_other(n):
            for gr, b in other[:n]:
                k = diff("S", 1, gr, b, 128 - 128 * b)
                o = 1024 * (gr // 2) + 512 - 512 * b
                act(T.m2[:, o + 2 * (gr % 2) + 1:o + 512:4], bank(k, 128), F.Sign, [("K", k)], [("m2", gr, b, 1)],
                    bias=(1 - 2 * b) * 2.0 ** -120)
            del other[:n]

        def sign(h, k):
            c = 128 * (k % 2) + 16 * (4 * h + k // 2)
            for a, n in ((0, 1), (1, 1)) if h + k == 0 else ((0, 2),):
                act(T.dd[:, 1024 * k + 512 * a:1024 * k + 512 * (a + n)], T["pr%d" % h][:, 512 * a:512 * (a + n)], F.Sign,
                    [("K", 2 * h + i) for i in range(a, a + n)] + [("cols", k % 2)], [("dd", k, i) for i in range(a, a + n)],
                    scale=-1.0, bias=T.cols[:, c:c + 1])

        def fix(h, k):
            b, tq, base, dg = k % 2, k % 4, 4096 * (k // 4), 128 * k
            dk = [("dd", k, 0), ("dd", k, 1)]
            if dg:
                ts(T.mt[:, base + tq:base + 4 * dg:4], T.dd[:, 1024 * k:1024 * k + dg], 0.0, A.is_gt, dk, [("mt", k, 0)])
            if dg + 128 < 1024:
                ts(T.mt[:, base + 4 * (dg + 128) + tq:base + 4096:4], T.dd[:, 1024 * k + dg + 128:1024 * k + 1024], 0.0, A.is_ge, dk, [("mt", k, 1)])
            kk = diff("V", 0, 4 * h + k // 2, b, 128 * b)
            tt(T.mt[:, base + 4 * dg + tq:base + 4 * (dg + 128):4], bank(kk, 128), T["thr%d" % b][:, 128 * b:128 * b + 128], A.is_gt,
               [("K", kk), "thr%d" % b], [("mt", k, 2)])

        def qm(h, i):
            m0 = 1024 * (2 * h + i)
            for a in (0, 512):
                quant("mq", m0 + a, m0 + a + 512, "mt", ("mq", h, i, a), [("mt", k, e) for k in range(4 * i, 4 * i + 4) for e in range(3)],
                      s0=4096 * i + 4 * a)

        def count(h, i, gis, first=False, last=False):
            m0 = 1024 * (2 * h + i)
            for gi in gis:
                gr = 4 * h + gi
                mk = [("mq", h, i, 512 * (gi // 2)), "cc0", "cc1"]
                if gi // 2 == i:
                    mm(1, 256, "cc", 256 * (1 + gi % 2) + 112 - 16 * gr, "mq", m0 + 256 * gi, first and gi % 2 == 0, last and gi % 2 == 1, mk)
            for gi in gis:
                gr = 4 * h + gi
                mk = [("mq", h, i, 512 * (gi // 2)), "cc0", "cc1"]
                mm(0, 256, "cc", 112 - 16 * gr, "mq", m0 + 256 * gi, first and gi == 0, last and gi == 3, mk)

        wins = [(s, b) for s in range(4) for b in range(4)] + [(4, b) for b in range(4)]
        wn = [0]
        pend = []

        def win_mm(n):
            for _i in range(n):
                if wins:
                    s, b = wins.pop(0)
                    k = (7, 2, 3, 5, 6)[wn[0] % 5]
                    wn[0] += 1
                    if s < 4:
                        mm(k, 256, "cwn", 128 * (4 * s + b), land, 0, True, True, [land, ("cwn", s, b)])
                    else:
                        mm(k, 256, "cid", 128 * b, qx, 256, True, True, [X, ("cid", b)])
                    pend.append((k, s, b))

        def win_cp(n):
            for _i in range(n):
                if pend:
                    k, s, b = pend.pop(0)
                    if s < 4:
                        o = 1024 * b + 256 * s
                        act(T.win[:, o:o + 256], bank(k, 256), F.Copy, [("K", k)], [("win", s, b)])
                    else:
                        act(T.fx[:, b:1024:4], bank(k, 256), F.Copy, [("K", k)], [("fx", b)])

        if t == 0:
            rows(0, 1)
            sign(0, 0)
            pick_u(1024)
            s2_same(2)
            setup_cols()
            setup_windows((0, 1))
            setup_pool()
        else:
            s2_same(1)
            rows(0, 1)
            s2_same(1)
        for k in range(8):
            if t or k:
                sign(0, k)
            if t == 0 and k in (1, 2):
                pick_u(1024 * k - 512)
            s2_other(OTHER[0][k])
            if k in (2, 4):
                rows(1, k // 2 - 1)
            s2_same(SAME[0][k])
            fix(0, k)
            if t == 0 and 2 < k < 7:
                (setup_ones, lambda: setup_windows((2,)), lambda: setup_windows((3,)), setup_own)[k - 3]()
            if k % 4 == 3:
                qm(0, k // 4)
        if t == 0:
            setup_lists()
        for k in range(8):
            sign(1, k)
            s2_other(OTHER[1][k])
            s2_same(SAME[1][k])
            fix(1, k)
            if k == 1:
                for a in (0, 512):
                    quant("m2q", a, a + 512, "m2", ("m2q", a), s2k, s0=4 * a)
            if k == 2:
                for q in range(4):
                    mm(4, 256, "cc", 768 + 112 - 32 * q, "m2q", 256 * q, q == 0, q == 3, [("m2q", 512 * (q // 2)), "cc1"])
            if k == 3:
                count(0, 0, range(4), True)
                qm(1, 0)
                wrap(bank(4, 256), "mk16", "rs16", [("K", 4)])
                ts(T.n2l[:], T.scn[:, 15:256:16], 64.0, A.add, ["scn"], ["n2l"])
                vcopy(T.leaf[:, 0:256].indirect(T.n2l[:, 0:16]), T.itb[:], ["itb", "n2l"], ["leaf"])
                dmas("Y", [(T.ld[16 * (q // 4):16 * (q // 4) + 16, 256 * (q % 4):256 * (q % 4) + 256], T.leaf[16 * q:16 * q + 16, :]) for q in range(8)], ["leaf"], ["ld"])
                dmas("Y", [(T.lw[16 * q:16 * q + 16, :], T.ld[16 * (q % 2):16 * (q % 2) + 16, :]) for q in range(8)], ["ld"], ["lw"])
            if k == 4:
                count(0, 1, range(4))
            if k == 5:
                count(1, 0, range(4))
        qm(1, 1)
        win_mm(3)
        count(1, 1, (0, 1))
        win_cp(3)
        count(1, 1, (2, 3), last=True)

        act(T.ab[:], bank(1, 256), F.Copy, [("K", 1)], ["ab"], scale=0.03125, bias=191.515625)
        act(T.da[:], T.ab[:], F.Identity, ["ab", "kc10", "kc11"], ["da"], scale=kc(11), bias=kc(10))
        act(T.dn[:], bank(1, 256), F.Copy, [("K", 1), "cf"], ["dn"], scale=col(5))
        wrap(bank(0, 256), "mk16", "rs16", [("K", 0)])
        vcopy(T.pl[:], T.scn[:, 15:256:16], ["scn"], ["pl"])
        tt(T.dat[:], T.dn[:], T.da[:], A.add, ["dn", "da"], ["dat"])
        vcopy(T.ww[:, 0:1024].indirect(T.pl[:, 0:16]), T.dat[:], ["pl", "dat"], ["ww"])
        quant("qw", 0, 256, "ww", "qw", ["ww"])
        win_mm(5)
        mm(4, 256, "ke", 0, "qw", 0, True, True, ["ke", "qw"])
        win_cp(5)
        while wins or pend:
            win_mm(3)
            win_cp(3)
        wrap(bank(4, 256), "mk16", "rs16", [("K", 4)])
        ts(T.ql[:], T.scn[:, 15:256:16], 528.0, A.add, ["scn"], ["ql"])
        wrap(T.lw[:, 0:1024].indirect(T.ql[:, 0:16]), "mk4", "rs4", ["lw", "ql"])
        el = "el%d" % t
        ts(T[el][:], T.scn[:, 3:256:4], kc(6), A.add, ["scn", "kc6"], [el])
        remote(T[lin][:], T[el][:], "lst%d" % t, [el])

        wrap(bank(1, 256), "mk16", "rs16", [("K", 1)])
        vcopy(T.n1l[:], T.scn[:, 15:256:16], ["scn"], ["n1l"])
        vcopy(T.psb[:], bank(0, 256), [("K", 0)], ["psb"])
        vcopy(T.awin[:, 0:256].indirect(T.n1l[:, 0:16]), T.psb[:], ["n1l", "psb"], ["awin"])
        wrap(T.awin[:, 0:256].indirect(T.n2l[:, 0:16]), "mk4", "rs4", ["awin", "n2l"])
        if t == R - 1:
            vcopy(T.dfull[:], T.awin[:, 0:256].indirect(T.n2l[:, 0:16]), ["awin", "n2l"], ["dfull"])
            ts(T.dfull[:], T.dfull[:], 2.0, A.mult, ["dfull", "cf"], ["dfull"], col(6), A.add)
            dmas("Y", [(T.op[q:q + 1, :], T.dfull[16 * q:16 * q + 1, :]) for q in range(8)], ["dfull"], ["op"])
            quant("qv", 0, 128, "vb", "qv", ["vb"])
        if t == 0:
            vcopy(T.qwr[:].bitcast(dt.uint32), T.wq[:, 0:512].bitcast(dt.uint32).indirect(T.wlist[:, 0:128]), ["wq", "wlist"], ["qwr"])
            act(T.qwr_s[:], T.wq_s[:, 0:512].indirect(T.wlist[:, 0:128]), F.Copy, ["wqs", "wlist"], ["qwrs"])

        wk = [("win", s, b) for s in range(4) for b in range(4)] + [lin]
        for i in range(2):
            act(T.etmp[:, 256 * i:256 * i + 256], T.win[:, 0:4096].indirect(T[lin][:, 16 * i:16 * i + 16]), F.Copy, wk, [("etmp", i)])
            tt(T.eb[:, 256 * i:256 * i + 256], T.win[:, 0:4096].indirect(T[lin][:, 32 + 16 * i:48 + 16 * i]), T.etmp[:, 256 * i:256 * i + 256], A.add,
               wk + [("etmp", i)], [("eb", i)])
        quant("qe", 0, 128, "eb", "qe", [("eb", 0), ("eb", 1)])
        vcopy(T.xi[:], T.scn[:, 3:256:4], ["scn"], ["xi"])
        ts(T.xi2[:], T.xi[:], 2, A.logical_shift_right, ["xi"], ["xi2"], 127, A.bitwise_and)
        ts(T.xi3[:], T.xi[:], 3, A.bitwise_and, ["xi"], ["xi3"])
        ts(T.xi3[:], T.xi3[:], 128.0, A.mult, ["xi3", "kc7"], ["xi3"], kc(7), A.add)
        tt(T.xi2[:], T.xi2[:], T.xi3[:], A.add, ["xi2", "xi3"], ["xi2"])
        vcopy(T.xl[:], T.xi2[:], ["xi2"], ["xl"])
        for i in range(16):
            k, s, b = i % 8, i // 4, i % 4
            mm(k, 128, "qwr", 128 * (4 * b + s), "qe", 0, True, True, ["qwr", "qwrs", "qe"])
            o = 512 * b + 128 * s
            if i % 2:
                ts(T.winh[:, o:o + 128], bank(k, 128), 0.015625, A.mult, [("K", k)], [("winh", i)])
            else:
                act(T.winh[:, o:o + 128], bank(k, 128), F.Copy, [("K", k)], [("winh", i)], scale=0.015625)
        hk = [("winh", i) for i in range(16)] + ["xl"] + [("fx", b) for b in range(4)]
        for i in range(2):
            c = 512 * i
            tt(T.xs[:, c:c + 512], T.winh[:, 0:2048].indirect(T.xl[:, 32 * i:32 * i + 32]), T.fx[:, c:c + 512], A.add, hk, [("xs", i)])
            if t < R - 1:
                act(T.xn[:, c:c + 512], T.xs[:, c:c + 512], F.Copy, [("xs", i)], [("xn", i), "xn"] if t == 0 else [("xn", i)], scale=-1.0)
        if t < R - 1:
            quant("qx%d" % (t + 1), 256, 512, "xs", ("qx", t + 1), [("xs", 0), ("xs", 1)])
        else:
            quant("qx3", 0, 256, "xs", "qx3", [("xs", 0), ("xs", 1)])

    mm(0, 256, "qv", 0, "qx3", 0, True, True, ["qv", "qx3"])
    dmas("Y", [(T.oc[:, :], cv("qx3", 0, 256))], ["qx3"], ["oc"])
    dmas("S", [(T.osc[4 * k:4 * k + 4, :], T.qx3_s[32 * k:32 * k + 4, 0:256]) for k in range(4)], ["qx3"], ["osc"])
    vcopy(T.ysb[:], bank(0, 256), [("K", 0)], ["ysb"])
    dmas("Y", [(T.y[:, :], T.ysb[:])], ["ysb"], ["y"])
    total["ls"] = nrem[0] * n_eng
    for e in cnt:
        total["s" + e] = cnt[e]
    for s in sorted(total):
        g.wait_ge(T.sem[s], total[s])
